import numpy as np, ml_dtypes
CORES = [35,38,43,46]
N = 4
import mx_ref
NC = 192
BF = ml_dtypes.bfloat16
def cut(t, i, w=512):
    return t[:, w * i:w * i + w]
def tile(rs):
    return np.stack(rs, axis=2).reshape(128, -1).astype(BF)
def onehot(t, r):
    own, p, b = t[:, :NC], t[:, NC:2 * NC], t[:, 2 * NC:]
    return tile([((own == r) & (p == np.arange(128)[:, None]) & (b == f)).astype(np.float32) for f in range(4)])
def setup_inputs(rng):
    def f(*shape):
        return mx_ref.flush((rng.standard_normal(shape, dtype=np.float32) * np.exp2(rng.integers(-2, 3, shape[:-1] + (1,)))).astype(BF))
    t = np.concatenate([rng.integers(0, N, (N, 1, NC)), rng.integers(0, 128, (N, 1, NC)), rng.integers(0, 4, (N, 1, NC))], axis=2)
    return {"tg": np.broadcast_to(t, (N, 128, 3 * NC)).astype(BF).copy(), "tab": f(N, 128, 4 * 512), "w": f(N, 128, 512)}
def setup_inputs_blocks(rng):
    d = setup_inputs(rng)
    for k in ("tab", "w"): d[k] = mx_ref.spread(d[k], rng, 4)
    return d
def setup_inputs_wide(rng):
    d = setup_inputs(rng)
    for k in ("tab", "w"): d[k] = mx_ref.flush((d[k].astype(np.float32) * np.exp2(rng.integers(-6, 7, (N, 1, 1))).astype(np.float32)).astype(BF))
    return d
def setup_inputs_hot(rng):
    d = setup_inputs(rng); t = d["tg"].astype(np.float32); t[:, :, :NC] = rng.integers(0, N); t[:, :, NC:2 * NC] = np.broadcast_to(rng.integers(0, 4, (N, 1, NC)), (N, 128, NC))
    d["tg"] = t.astype(BF)
    return d
def reference(tg, tab, w):
    y = np.zeros((N, 128, NC), np.float32)
    for j in range(N):
        qw = mx_ref.quantize(w[j])
        for r in range(N):
            o = mx_ref.quantize(onehot(tg[j].astype(np.float32), r))
            e = mx_ref.quantize(tile([mx_ref.matmul(mx_ref.quantize(cut(tab[r], f)), o) for f in range(4)]))
            p = mx_ref.matmul(qw, e)
            y[j] = p if r == 0 else y[j] + p
    return {"y": y}

@@ -1,0 +1,169 @@
+from concourse.bass import DstId, RemoteDMATransfer
+from concourse.mybir import AluOpType, ActivationFunctionType, dt
+
+NC = 192
+SCRATCH = {
+    "xo": ("sbuf", [128, 6], "bfloat16"), "xp": ("sbuf", [128, 6], "bfloat16"), "xb": ("sbuf", [128, 6], "bfloat16"),
+    "t1": ("sbuf", [128, 6], "float32"), "t2": ("sbuf", [128, 6], "float32"), "t3": ("sbuf", [128, 6], "float32"),
+    "e6": ("sbuf", [128, 6], "float32"), "es": ("sbuf", [128, 3], "float32"),
+    "keys": ("sbuf", [128, 9], "bfloat16"), "land": ("sbuf", [128, 9], "bfloat16"),
+    "msk": ("sbuf", [128, NC], "bfloat16"), "sel": ("sbuf", [128, 4], "bfloat16"),
+    "z": ("sbuf", [128, 4 * NC], "bfloat16"), "zs": ("sbuf", [128, 4 * NC], "bfloat16"), "kb": ("sbuf", [128, 4 * NC], "bfloat16"),
+    "tabs": ("sbuf", [128, 2048], "bfloat16"), "tabc": ("sbuf", [128, 512], "float8_e4m3fn_x4"), "tabp": ("sbuf", [128, 512], "uint8"),
+    "wsb": ("sbuf", [128, 512], "bfloat16"), "wc": ("sbuf", [128, 128], "float8_e4m3fn_x4"), "wp": ("sbuf", [128, 128], "uint8"),
+    "o": ("sbuf", [128, 16 * NC], "bfloat16"), "oc": ("sbuf", [128, 4 * NC], "float8_e4m3fn_x4"), "op": ("sbuf", [128, 4 * NC], "uint8"),
+    "e": ("sbuf", [128, 16 * NC], "bfloat16"), "ec": ("sbuf", [128, 4 * NC], "float8_e4m3fn_x4"), "ep": ("sbuf", [128, 4 * NC], "uint8"),
+    "lc": ("sbuf", [128, 3 * NC], "float8_e4m3fn_x4"), "lp": ("sbuf", [128, 3 * NC], "uint8"),
+    "ysb": ("sbuf", [128, NC], "float32"),
+    "zp": ("psum", [128, 7 * 512], "float32"), "yp": ("psum", [128, 512], "float32"),
+}
+SEMAPHORES = ["x", "tl0", "tl1", "tl2", "tl3", "wl", "vs", "ps", "ss", "gs", "ids", "el0", "el1", "el2", "left", "st"]
+A = AluOpType
+
+
+def rank_program(g, core, T, topo):
+    rank = T.rank_of(core)
+    if rank is None:
+        return
+
+    others = sorted((r for r in range(len(T.cores)) if r != rank),
+                    key=lambda r: (topo.chip(T.cores[r]) == topo.chip(core), topo.die(T.cores[r]) != topo.die(core)))
+    dests = [T.cores[r] for r in others]
+    bits = lambda m: [1 << i for i in range(m.bit_length()) if m >> i & 1]
+    off = [d for d in dests if topo.chip(d) != topo.chip(core)]
+    far = bits(topo.mask(core, off[0]))
+    near = [b for b in bits(topo.mask(core, dests[-1])) if b not in far]
+    share = len(far) // len(off)
+    id_eng = [far[share * i:share * i + share] for i in range(len(off))] + [near]
+    e_eng = [far] * len(off) + [near]
+
+    seen, n = {}, {"vs": 0}
+
+    def need(q, name, *deps):
+        for sem, val in deps:
+            if seen.get((name, sem), 0) < val:
+                q.wait_ge(T.sem[sem], val)
+                seen[(name, sem)] = val
+
+    def vec(call, *args, after=()):
+        need(g.vector, "v", *after)
+        call(*args).then_inc(T.sem.vs, 1)
+        n["vs"] += 1
+        return ("vs", n["vs"])
+
+    v = g.vector
+
+    g.sync.dma_start(T.xp[:], T.tg[0:4, NC:2 * NC]).then_inc(T.sem.x, 16)
+    g.scalar.dma_start(T.xo[:], T.tg[0:4, 0:NC]).then_inc(T.sem.x, 16)
+    g.sync.dma_start(T.xb[:], T.tg[0:4, 2 * NC:3 * NC]).then_inc(T.sem.x, 16)
+    for f in range(4):
+        q = g.scalar if f % 2 == 0 else g.sync
+        q.dma_start(T.tabs[:, 512 * f:512 * f + 512], T.tab[:, 512 * f:512 * f + 512]).then_inc(T.sem["tl%d" % f], 16)
+    g.sync.dma_start(T.wsb[:], T.w[:]).then_inc(T.sem.wl, 16)
+
+    g.iota(T.sel[:], [[1, 4]], -256, 4, allow_small_or_imprecise_dtypes=True).then_inc(T.sem.gs, 1)
+    m1 = vec(v.memset, T.msk[:], 1.0)
+    m2 = vec(v.memset, T.z[:], 0.0)
+    m3 = vec(v.memset, T.msk[:, 0:NC:32], 0.0, after=[m1])
+
+    a1 = vec(v.tensor_scalar, T.t1[:], T.xp[:], 4.0, -256.0, A.mult, A.add, after=[("x", 48)])
+    a2 = vec(v.tensor_scalar, T.t2[:], T.xo[:], 1024.0, None, A.mult)
+    a3 = vec(v.tensor_tensor, T.t3[:], T.t1[:], T.xb[:], A.add, after=[a1])
+    vec(v.tensor_tensor, T.es[0:64, :], T.t3[0:64, 0:6:2], T.t2[0:64, 0:6:2], A.add, after=[a3])
+    a5 = vec(v.tensor_tensor, T.es[64:128, :], T.t3[64:128, 1:6:2], T.t2[64:128, 1:6:2], A.add)
+    for s, r in enumerate(others):
+        sent = vec(v.tensor_scalar, T.keys[:, 3 * s:3 * s + 3], T.es[:], -1024.0 * r, None, A.add, after=[a5])
+    need(g, "g", sent)
+    g.remote_dma_fused([RemoteDMATransfer(dst_ids=[DstId(rid=topo.addr(d)[0], pnc=topo.addr(d)[1])], dma_engine_mask=sum(id_eng[s]),
+                                          remote_sem=T.sem.ids, src=T.keys[:, 3 * s:3 * s + 3], dst=T.land[:, 3 * s:3 * s + 3])
+                        for s, d in enumerate(dests)], local_sem=T.sem.left)
+
+    sl = lambda s: slice(NC * s, NC * s + NC)
+    scan = lambda s, d: vec(v.tensor_tensor_scan, T.zs[:, sl(s)], T.msk[:], T.z[:, sl(s)], 0.0, A.mult, A.add, after=[m3, d])
+    turn = lambda s, d: vec(v.transpose, T.kb[:, sl(s)], T.zs[:, sl(s)], after=[d])
+
+    def compare(s, d):
+        for b in range(4):
+            last = vec(v.tensor_scalar, T.o[:, 768 * s + b:768 * s + 768:4], T.kb[:, sl(s)], T.sel[:, b:b + 1], None, A.is_equal, after=[d, ("gs", 1)])
+        return last
+
+    qo = lambda s, d: vec(v.quantize_mx, T.oc[:, sl(s)], T.op[:, sl(s)], T.o[:, 768 * s:768 * s + 768], after=[d])
+    qe = lambda s, *d: vec(v.quantize_mx, T.ec[:, sl(s)], T.ep[:, sl(s)], T.e[:, 768 * s:768 * s + 768], after=d)
+
+    b1 = vec(v.tensor_tensor, T.e6[:], T.t3[:], T.t2[:], A.add)
+    b2 = vec(v.tensor_scalar, T.z[:, 3 * NC:4 * NC:32], T.e6[:], -1024.0 * rank, None, A.add, after=[m2, b1])
+    o_done, tab_done = {}, []
+    o_done[3] = qo(3, compare(3, turn(3, scan(3, b2))))
+    for f in range(4):
+        tab_done.append(vec(v.quantize_mx, T.tabc[:, 128 * f:128 * f + 128], T.tabp[:, 128 * f:128 * f + 128],
+                            T.tabs[:, 512 * f:512 * f + 512], after=[("tl%d" % f, 16)]))
+
+    H, W9 = (slice(0, 64), slice(64, 128)), 3 * NC
+    arrived = ("ids", sum(len(x) for x in id_eng))
+    for here, there in ((0, 0), (1, 1), (0, 1), (1, 0)):
+        c = vec(v.tensor_copy, T.z[H[here], 32 * there:W9:64], T.land[H[there], :], after=[arrived])
+    s0 = scan(0, c)
+    s1 = scan(1, c)
+    c0 = compare(0, turn(0, s0))
+    s2 = scan(2, c)
+    o_done[0] = qo(0, c0)
+    c1 = compare(1, turn(1, s1))
+    k2 = turn(2, s2)
+    o_done[1] = qo(1, c1)
+
+    order = (3, 0, 1, 2)
+    e_copies = {}
+
+    def product(m):
+        s, f = order[m // 4], m % 4
+        need(g.tensor, "t", tab_done[f], o_done[s])
+        if m >= 7:
+            need(g.tensor, "t", ("ss", m - 6))
+        bank = 512 * (m % 7)
+        g.tensor.matmul_mx(T.zp[:, bank:bank + NC], T.tabc[:, 128 * f:128 * f + 128], T.tabp[:, 128 * f:128 * f + 128],
+                           T.oc[:, sl(s)], T.op[:, sl(s)], True, True).then_inc(T.sem.ps, 1)
+
+    def sides(m):
+        s, f, bank = order[m // 4], m % 4, 512 * (m % 7)
+        return T.e[:, 768 * s + f:768 * s + 768:4], T.zp[:, bank:bank + NC]
+
+    scalar_calls = [m for m in range(16) if m not in (13, 15)]
+    for i, m in enumerate(scalar_calls):
+        out, in_ = sides(m)
+        need(g.scalar, "s", ("ps", m + 1))
+        g.scalar.activation(out, in_, ActivationFunctionType.Copy).then_inc(T.sem.ss, 1)
+        e_copies[m // 4] = ("ss", i + 1)
+
+    e_done = {}
+    e_done[0] = qe(0, e_copies[1])
+    o_done[2] = qo(2, compare(2, k2))
+    e_done[1] = qe(1, e_copies[2])
+    for m in (13, 15):
+        out, in_ = sides(m)
+        mine = vec(v.tensor_copy, out, in_, after=[("ps", m + 1)])
+    e_done[2] = qe(2, e_copies[3], mine)
+    w_done = vec(v.quantize_mx, T.wc[:], T.wp[:], T.wsb[:], after=[("wl", 16)])
+    e_done[3] = qe(3, e_copies[0])
+
+    for m in range(16):
+        product(m)
+
+    for s, d in enumerate(dests):
+        rid, pid = topo.addr(d)[:2]
+        need(g, "g", e_done[s])
+        g.remote_dma(T.lc[:, sl(s)].bitcast(dt.uint8), T.ec[:, sl(s)].bitcast(dt.uint8), T.sem["el%d" % s], T.sem.left, pid, rid, sum(e_eng[s]))
+        g.remote_dma(T.lp[:, sl(s)], T.ep[:, sl(s)], T.sem["el%d" % s], T.sem.left, pid, rid, sum(e_eng[s]))
+
+    need(g.tensor, "t", w_done, e_done[3])
+    g.tensor.matmul_mx(T.yp[:, 0:NC], T.wc[:], T.wp[:], T.ec[:, sl(3)], T.ep[:, sl(3)], True, False)
+    for s in range(3):
+        need(g.tensor, "t", ("el%d" % s, 2 * len(e_eng[s])))
+        mm = g.tensor.matmul_mx(T.yp[:, 0:NC], T.wc[:], T.wp[:], T.lc[:, sl(s)], T.lp[:, sl(s)], False, s == 2)
+    mm.then_inc(T.sem.ps, 1)
+
+    for k in range(6):
+        fin = vec(v.tensor_copy, T.ysb[:, k:NC:6], T.yp[:, 32 * k:32 * k + 32], after=[("ps", 17)])
+    need(g.sync, "y", fin)
+    g.sync.dma_start(T.y[:], T.ysb[:]).then_inc(T.sem.st, 16)
+    g.sync.wait_ge(T.sem.st, 16)
+    g.wait_ge(T.sem.left, sum(len(x) for x in id_eng) + 2 * sum(len(x) for x in e_eng))

@@ -4,9 +4,10 @@ from concourse.mybir import AluOpType, ActivationFunctionType, dt
 NC = 192
 SCRATCH = {
     "xo": ("sbuf", [128, 6], "bfloat16"), "xp": ("sbuf", [128, 6], "bfloat16"), "xb": ("sbuf", [128, 6], "bfloat16"),
-    "t1": ("sbuf", [128, 6], "float32"), "t2": ("sbuf", [128, 6], "float32"), "t3": ("sbuf", [128, 6], "float32"),
-    "e6": ("sbuf", [128, 6], "float32"), "es": ("sbuf", [128, 3], "float32"),
-    "keys": ("sbuf", [128, 9], "bfloat16"), "land": ("sbuf", [128, 9], "bfloat16"),
+    "t1": ("sbuf", [128, 6], "float32"), "t2": ("sbuf", [128, 6], "float32"), "u2": ("sbuf", [128, 6], "float32"),
+    "t3": ("sbuf", [128, 6], "float32"), "u3": ("sbuf", [128, 6], "float32"), "e6": ("sbuf", [128, 6], "float32"),
+    "key0": ("sbuf", [128, 6], "bfloat16"), "key1": ("sbuf", [128, 6], "bfloat16"), "key2": ("sbuf", [128, 3], "bfloat16"),
+    "land0": ("sbuf", [128, 6], "bfloat16"), "land1": ("sbuf", [128, 6], "bfloat16"), "land2": ("sbuf", [128, 3], "bfloat16"),
     "msk": ("sbuf", [128, NC], "bfloat16"), "sel": ("sbuf", [128, 4], "bfloat16"),
     "z": ("sbuf", [128, 4 * NC], "bfloat16"), "zs": ("sbuf", [128, 4 * NC], "bfloat16"), "kb": ("sbuf", [128, 4 * NC], "bfloat16"),
     "tabs": ("sbuf", [128, 2048], "bfloat16"), "tabc": ("sbuf", [128, 512], "float8_e4m3fn_x4"), "tabp": ("sbuf", [128, 512], "uint8"),
@@ -17,7 +18,7 @@ SCRATCH = {
     "ysb": ("sbuf", [128, NC], "float32"),
     "zp": ("psum", [128, 7 * 512], "float32"), "yp": ("psum", [128, 512], "float32"),
 }
-SEMAPHORES = ["x", "tl0", "tl1", "tl2", "tl3", "wl", "vs", "ps", "ss", "gs", "ids", "el0", "el1", "el2", "left", "st"]
+SEMAPHORES = ["xo", "xp", "xb", "tl0", "tl1", "tl2", "tl3", "wl", "vs", "ps", "ss", "gs", "id0", "id1", "id2", "el0", "el1", "el2", "left", "st"]
 A = AluOpType
 
 
@@ -30,12 +31,10 @@ def rank_program(g, core, T, topo):
                     key=lambda r: (topo.chip(T.cores[r]) == topo.chip(core), topo.die(T.cores[r]) != topo.die(core)))
     dests = [T.cores[r] for r in others]
     bits = lambda m: [1 << i for i in range(m.bit_length()) if m >> i & 1]
-    off = [d for d in dests if topo.chip(d) != topo.chip(core)]
-    far = bits(topo.mask(core, off[0]))
+    far = bits(topo.mask(core, dests[0]))
     near = [b for b in bits(topo.mask(core, dests[-1])) if b not in far]
-    share = len(far) // len(off)
-    id_eng = [far[share * i:share * i + share] for i in range(len(off))] + [near]
-    e_eng = [far] * len(off) + [near]
+    eng = [far, far, near]
+    id_eng = [far[:len(far) // 2], far[len(far) // 2:], near]
 
     seen, n = {}, {"vs": 0}
 
@@ -53,63 +52,85 @@ def rank_program(g, core, T, topo):
 
     v = g.vector
 
-    g.sync.dma_start(T.xp[:], T.tg[0:4, NC:2 * NC]).then_inc(T.sem.x, 16)
-    g.scalar.dma_start(T.xo[:], T.tg[0:4, 0:NC]).then_inc(T.sem.x, 16)
-    g.sync.dma_start(T.xb[:], T.tg[0:4, 2 * NC:3 * NC]).then_inc(T.sem.x, 16)
+    g.sync.dma_start(T.xb[:], T.tg[0:4, 2 * NC:3 * NC]).then_inc(T.sem.xb, 16)
+    g.scalar.dma_start(T.xo[:], T.tg[0:4, 0:NC]).then_inc(T.sem.xo, 16)
+    g.sync.dma_start(T.xp[:], T.tg[0:4, NC:2 * NC]).then_inc(T.sem.xp, 16)
     for f in range(4):
-        q = g.scalar if f % 2 == 0 else g.sync
-        q.dma_start(T.tabs[:, 512 * f:512 * f + 512], T.tab[:, 512 * f:512 * f + 512]).then_inc(T.sem["tl%d" % f], 16)
+        g.sync.dma_start(T.tabs[:, 512 * f:512 * f + 512], T.tab[:, 512 * f:512 * f + 512]).then_inc(T.sem["tl%d" % f], 16)
     g.sync.dma_start(T.wsb[:], T.w[:]).then_inc(T.sem.wl, 16)
 
-    g.iota(T.sel[:], [[1, 4]], -256, 4, allow_small_or_imprecise_dtypes=True).then_inc(T.sem.gs, 1)
+    g.iota(T.sel[:], [[128, 4]], -256, 1, allow_small_or_imprecise_dtypes=True).then_inc(T.sem.gs, 1)
     m1 = vec(v.memset, T.msk[:], 1.0)
     m2 = vec(v.memset, T.z[:], 0.0)
     m3 = vec(v.memset, T.msk[:, 0:NC:32], 0.0, after=[m1])
 
-    a1 = vec(v.tensor_scalar, T.t1[:], T.xp[:], 4.0, -256.0, A.mult, A.add, after=[("x", 48)])
-    a2 = vec(v.tensor_scalar, T.t2[:], T.xo[:], 1024.0, None, A.mult)
-    a3 = vec(v.tensor_tensor, T.t3[:], T.t1[:], T.xb[:], A.add, after=[a1])
-    vec(v.tensor_tensor, T.es[0:64, :], T.t3[0:64, 0:6:2], T.t2[0:64, 0:6:2], A.add, after=[a3])
-    a5 = vec(v.tensor_tensor, T.es[64:128, :], T.t3[64:128, 1:6:2], T.t2[64:128, 1:6:2], A.add)
-    for s, r in enumerate(others):
-        sent = vec(v.tensor_scalar, T.keys[:, 3 * s:3 * s + 3], T.es[:], -1024.0 * r, None, A.add, after=[a5])
-    need(g, "g", sent)
-    g.remote_dma_fused([RemoteDMATransfer(dst_ids=[DstId(rid=topo.addr(d)[0], pnc=topo.addr(d)[1])], dma_engine_mask=sum(id_eng[s]),
-                                          remote_sem=T.sem.ids, src=T.keys[:, 3 * s:3 * s + 3], dst=T.land[:, 3 * s:3 * s + 3])
-                        for s, d in enumerate(dests)], local_sem=T.sem.left)
+    def send(s, dst, src, sem, *deps):
+        rid, pid = topo.addr(dests[s])[:2]
+        need(g, "g", *deps)
+        g.remote_dma(dst, src, T.sem[sem], T.sem.left, pid, rid, sum(eng[s]))
+
+    base = others[0]
+    shift = lambda r: 1024.0 * (base - r)
+    a1 = vec(v.tensor_scalar, T.t1[:], T.xb[:], 128.0, -256.0, A.mult, A.add, after=[("xb", 16)])
+    a2 = vec(v.tensor_scalar, T.t2[:], T.xo[:], 1024.0, -1024.0 * base, A.mult, A.add, after=[("xo", 16)])
+    b2 = vec(v.tensor_scalar, T.u2[:], T.xo[:], 1024.0, -1024.0 * others[1], A.mult, A.add)
+    a3 = vec(v.tensor_tensor, T.t3[:], T.t1[:], T.t2[:], A.add, after=[a1, a2])
+    b3 = vec(v.tensor_tensor, T.u3[:], T.t1[:], T.u2[:], A.add, after=[b2])
+    vec(v.tensor_tensor, T.key0[:], T.t3[:], T.xp[:], A.add, after=[a3, ("xp", 16)])
+    k1 = vec(v.tensor_tensor, T.key1[:], T.u3[:], T.xp[:], A.add, after=[b3])
+    a4 = vec(v.tensor_tensor, T.e6[:], T.t3[:], T.xp[:], A.add)
+    vec(v.tensor_scalar, T.key2[0:64, :], T.e6[0:64, 0:3], shift(others[2]), None, A.add, after=[a4])
+    k2 = vec(v.tensor_scalar, T.key2[64:128, :], T.e6[64:128, 3:6], shift(others[2]), None, A.add)
+    zown = vec(v.tensor_scalar, T.z[:, 3 * NC:4 * NC:32], T.e6[:], shift(rank), None, A.add, after=[m2])
+    need(g, "g", k1)
+    g.remote_dma_fused([RemoteDMATransfer(dst_ids=[DstId(rid=topo.addr(dests[s])[0], pnc=topo.addr(dests[s])[1])], dma_engine_mask=sum(id_eng[s]),
+                                          remote_sem=T.sem["id%d" % s], src=T["key%d" % s][:], dst=T["land%d" % s][:]) for s in (0, 1)], local_sem=T.sem.left)
+    send(2, T.land2[:], T.key2[:], "id2", k2)
 
     sl = lambda s: slice(NC * s, NC * s + NC)
     scan = lambda s, d: vec(v.tensor_tensor_scan, T.zs[:, sl(s)], T.msk[:], T.z[:, sl(s)], 0.0, A.mult, A.add, after=[m3, d])
     turn = lambda s, d: vec(v.transpose, T.kb[:, sl(s)], T.zs[:, sl(s)], after=[d])
 
-    def compare(s, d):
-        for b in range(4):
+    def compare(s, d, bs=(0, 1, 2, 3)):
+        for b in bs:
             last = vec(v.tensor_scalar, T.o[:, 768 * s + b:768 * s + 768:4], T.kb[:, sl(s)], T.sel[:, b:b + 1], None, A.is_equal, after=[d, ("gs", 1)])
         return last
 
     qo = lambda s, d: vec(v.quantize_mx, T.oc[:, sl(s)], T.op[:, sl(s)], T.o[:, 768 * s:768 * s + 768], after=[d])
     qe = lambda s, *d: vec(v.quantize_mx, T.ec[:, sl(s)], T.ep[:, sl(s)], T.e[:, 768 * s:768 * s + 768], after=d)
+    qt = lambda f: vec(v.quantize_mx, T.tabc[:, 128 * f:128 * f + 128], T.tabp[:, 128 * f:128 * f + 128],
+                       T.tabs[:, 512 * f:512 * f + 512], after=[("tl%d" % f, 16)])
+    place = lambda s: vec(v.tensor_copy, T.z[:, NC * s:NC * s + NC:32], T["land%d" % s][:], after=[m2, ("id%d" % s, len(id_eng[s]))])
 
-    b1 = vec(v.tensor_tensor, T.e6[:], T.t3[:], T.t2[:], A.add)
-    b2 = vec(v.tensor_scalar, T.z[:, 3 * NC:4 * NC:32], T.e6[:], -1024.0 * rank, None, A.add, after=[m2, b1])
-    o_done, tab_done = {}, []
-    o_done[3] = qo(3, compare(3, turn(3, scan(3, b2))))
-    for f in range(4):
-        tab_done.append(vec(v.quantize_mx, T.tabc[:, 128 * f:128 * f + 128], T.tabp[:, 128 * f:128 * f + 128],
-                            T.tabs[:, 512 * f:512 * f + 512], after=[("tl%d" % f, 16)]))
+    def place_half(here, there):
+        h = (slice(0, 64), slice(64, 128))
+        first = 2 * NC + 96 * there
+        return vec(v.tensor_copy, T.z[h[here], first:first + 96:32], T.land2[h[there], :], after=[("id2", len(id_eng[2]))])
 
-    H, W9 = (slice(0, 64), slice(64, 128)), 3 * NC
-    arrived = ("ids", sum(len(x) for x in id_eng))
-    for here, there in ((0, 0), (1, 1), (0, 1), (1, 0)):
-        c = vec(v.tensor_copy, T.z[H[here], 32 * there:W9:64], T.land[H[there], :], after=[arrived])
-    s0 = scan(0, c)
-    s1 = scan(1, c)
-    c0 = compare(0, turn(0, s0))
-    s2 = scan(2, c)
+    o_done, e_done = {}, {}
+    o_done[3] = qo(3, compare(3, turn(3, scan(3, zown))))
+    tab_done = [qt(f) for f in range(4)]
+
+    p0 = place(0)
+    p1 = place(1)
+    s0 = scan(0, p0)
+    s1 = scan(1, p1)
+    t0 = turn(0, s0)
+    t1 = turn(1, s1)
+    c0 = compare(0, t0)
+    compare(1, t1, (0,))
     o_done[0] = qo(0, c0)
-    c1 = compare(1, turn(1, s1))
-    k2 = turn(2, s2)
+    compare(1, t1, (1,))
+    place_half(0, 0)
+    place_half(1, 1)
+    place_half(0, 1)
+    p2 = place_half(1, 0)
+    compare(1, t1, (2,))
+    s2 = scan(2, p2)
+    c1 = compare(1, t1, (3,))
+    t2 = turn(2, s2)
     o_done[1] = qo(1, c1)
+    c2 = compare(2, t2)
 
     order = (3, 0, 1, 2)
     e_copies = {}
@@ -134,9 +155,8 @@ def rank_program(g, core, T, topo):
         g.scalar.activation(out, in_, ActivationFunctionType.Copy).then_inc(T.sem.ss, 1)
         e_copies[m // 4] = ("ss", i + 1)
 
-    e_done = {}
     e_done[0] = qe(0, e_copies[1])
-    o_done[2] = qo(2, compare(2, k2))
+    o_done[2] = qo(2, c2)
     e_done[1] = qe(1, e_copies[2])
     for m in (13, 15):
         out, in_ = sides(m)
@@ -148,16 +168,14 @@ def rank_program(g, core, T, topo):
     for m in range(16):
         product(m)
 
-    for s, d in enumerate(dests):
-        rid, pid = topo.addr(d)[:2]
-        need(g, "g", e_done[s])
-        g.remote_dma(T.lc[:, sl(s)].bitcast(dt.uint8), T.ec[:, sl(s)].bitcast(dt.uint8), T.sem["el%d" % s], T.sem.left, pid, rid, sum(e_eng[s]))
-        g.remote_dma(T.lp[:, sl(s)], T.ep[:, sl(s)], T.sem["el%d" % s], T.sem.left, pid, rid, sum(e_eng[s]))
+    for s in range(3):
+        send(s, T.lc[:, sl(s)].bitcast(dt.uint8), T.ec[:, sl(s)].bitcast(dt.uint8), "el%d" % s, e_done[s])
+        send(s, T.lp[:, sl(s)], T.ep[:, sl(s)], "el%d" % s)
 
     need(g.tensor, "t", w_done, e_done[3])
     g.tensor.matmul_mx(T.yp[:, 0:NC], T.wc[:], T.wp[:], T.ec[:, sl(3)], T.ep[:, sl(3)], True, False)
     for s in range(3):
-        need(g.tensor, "t", ("el%d" % s, 2 * len(e_eng[s])))
+        need(g.tensor, "t", ("el%d" % s, 2 * len(eng[s])))
         mm = g.tensor.matmul_mx(T.yp[:, 0:NC], T.wc[:], T.wp[:], T.lc[:, sl(s)], T.lp[:, sl(s)], False, s == 2)
     mm.then_inc(T.sem.ps, 1)
 
@@ -166,4 +184,4 @@ def rank_program(g, core, T, topo):
     need(g.sync, "y", fin)
     g.sync.dma_start(T.y[:], T.ysb[:]).then_inc(T.sem.st, 16)
     g.sync.wait_ge(T.sem.st, 16)
-    g.wait_ge(T.sem.left, sum(len(x) for x in id_eng) + 2 * sum(len(x) for x in e_eng))
+    g.wait_ge(T.sem.left, sum(len(x) for x in id_eng) + 2 * sum(len(x) for x in eng))

from concourse.bass import DstId, RemoteDMATransfer
from concourse.mybir import AluOpType, ActivationFunctionType, dt

NC = 192
SCRATCH = {
    "xo": ("sbuf", [128, 6], "bfloat16"), "xp": ("sbuf", [128, 6], "bfloat16"), "xb": ("sbuf", [128, 6], "bfloat16"),
    "t1": ("sbuf", [128, 6], "float32"), "t2": ("sbuf", [128, 6], "float32"), "u2": ("sbuf", [128, 6], "float32"),
    "t3": ("sbuf", [128, 6], "float32"), "u3": ("sbuf", [128, 6], "float32"), "e6": ("sbuf", [128, 6], "float32"),
    "key0": ("sbuf", [128, 6], "bfloat16"), "key1": ("sbuf", [128, 6], "bfloat16"), "key2": ("sbuf", [128, 3], "bfloat16"),
    "land0": ("sbuf", [128, 6], "bfloat16"), "land1": ("sbuf", [128, 6], "bfloat16"), "land2": ("sbuf", [128, 3], "bfloat16"),
    "msk": ("sbuf", [128, NC], "bfloat16"), "sel": ("sbuf", [128, 4], "bfloat16"),
    "z": ("sbuf", [128, 4 * NC], "bfloat16"), "zs": ("sbuf", [128, 4 * NC], "bfloat16"), "kb": ("sbuf", [128, 4 * NC], "bfloat16"),
    "tabs": ("sbuf", [128, 2048], "bfloat16"), "tabc": ("sbuf", [128, 512], "float8_e4m3fn_x4"), "tabp": ("sbuf", [128, 512], "uint8"),
    "wsb": ("sbuf", [128, 512], "bfloat16"), "wc": ("sbuf", [128, 128], "float8_e4m3fn_x4"), "wp": ("sbuf", [128, 128], "uint8"),
    "o": ("sbuf", [128, 16 * NC], "bfloat16"), "oc": ("sbuf", [128, 4 * NC], "float8_e4m3fn_x4"), "op": ("sbuf", [128, 4 * NC], "uint8"),
    "e": ("sbuf", [128, 16 * NC], "bfloat16"), "ec": ("sbuf", [128, 4 * NC], "float8_e4m3fn_x4"), "ep": ("sbuf", [128, 4 * NC], "uint8"),
    "lc": ("sbuf", [128, 3 * NC], "float8_e4m3fn_x4"), "lp": ("sbuf", [128, 3 * NC], "uint8"),
    "ysb": ("sbuf", [128, NC], "float32"),
    "zp": ("psum", [128, 7 * 512], "float32"), "yp": ("psum", [128, 512], "float32"),
}
SEMAPHORES = ["xo", "xp", "xb", "tl0", "tl1", "tl2", "tl3", "wl", "vs", "ps", "ss", "gs", "id0", "id1", "id2", "el0", "el1", "el2", "left", "st"]
A = AluOpType


def rank_program(g, core, T, topo):
    rank = T.rank_of(core)
    if rank is None:
        return

    others = sorted((r for r in range(len(T.cores)) if r != rank),
                    key=lambda r: (topo.chip(T.cores[r]) == topo.chip(core), topo.die(T.cores[r]) != topo.die(core)))
    dests = [T.cores[r] for r in others]
    bits = lambda m: [1 << i for i in range(m.bit_length()) if m >> i & 1]
    far = bits(topo.mask(core, dests[0]))
    near = [b for b in bits(topo.mask(core, dests[-1])) if b not in far]
    eng = [far, far, near]
    id_eng = [far[:len(far) // 2], far[len(far) // 2:], near]

    seen, n = {}, {"vs": 0}

    def need(q, name, *deps):
        for sem, val in deps:
            if seen.get((name, sem), 0) < val:
                q.wait_ge(T.sem[sem], val)
                seen[(name, sem)] = val

    def vec(call, *args, after=()):
        need(g.vector, "v", *after)
        call(*args).then_inc(T.sem.vs, 1)
        n["vs"] += 1
        return ("vs", n["vs"])

    v = g.vector

    g.sync.dma_start(T.xb[:], T.tg[0:4, 2 * NC:3 * NC]).then_inc(T.sem.xb, 16)
    g.scalar.dma_start(T.xo[:], T.tg[0:4, 0:NC]).then_inc(T.sem.xo, 16)
    g.sync.dma_start(T.xp[:], T.tg[0:4, NC:2 * NC]).then_inc(T.sem.xp, 16)
    for f in range(4):
        g.sync.dma_start(T.tabs[:, 512 * f:512 * f + 512], T.tab[:, 512 * f:512 * f + 512]).then_inc(T.sem["tl%d" % f], 16)
    g.sync.dma_start(T.wsb[:], T.w[:]).then_inc(T.sem.wl, 16)

    g.iota(T.sel[:], [[128, 4]], -256, 1, allow_small_or_imprecise_dtypes=True).then_inc(T.sem.gs, 1)
    m1 = vec(v.memset, T.msk[:], 1.0)
    m2 = vec(v.memset, T.z[:], 0.0)
    m3 = vec(v.memset, T.msk[:, 0:NC:32], 0.0, after=[m1])

    def send(s, dst, src, sem, *deps):
        rid, pid = topo.addr(dests[s])[:2]
        need(g, "g", *deps)
        g.remote_dma(dst, src, T.sem[sem], T.sem.left, pid, rid, sum(eng[s]))

    base = others[0]
    shift = lambda r: 1024.0 * (base - r)
    a1 = vec(v.tensor_scalar, T.t1[:], T.xb[:], 128.0, -256.0, A.mult, A.add, after=[("xb", 16)])
    a2 = vec(v.tensor_scalar, T.t2[:], T.xo[:], 1024.0, -1024.0 * base, A.mult, A.add, after=[("xo", 16)])
    b2 = vec(v.tensor_scalar, T.u2[:], T.xo[:], 1024.0, -1024.0 * others[1], A.mult, A.add)
    a3 = vec(v.tensor_tensor, T.t3[:], T.t1[:], T.t2[:], A.add, after=[a1, a2])
    b3 = vec(v.tensor_tensor, T.u3[:], T.t1[:], T.u2[:], A.add, after=[b2])
    vec(v.tensor_tensor, T.key0[:], T.t3[:], T.xp[:], A.add, after=[a3, ("xp", 16)])
    k1 = vec(v.tensor_tensor, T.key1[:], T.u3[:], T.xp[:], A.add, after=[b3])
    a4 = vec(v.tensor_tensor, T.e6[:], T.t3[:], T.xp[:], A.add)
    vec(v.tensor_scalar, T.key2[0:64, :], T.e6[0:64, 0:3], shift(others[2]), None, A.add, after=[a4])
    k2 = vec(v.tensor_scalar, T.key2[64:128, :], T.e6[64:128, 3:6], shift(others[2]), None, A.add)
    zown = vec(v.tensor_scalar, T.z[:, 3 * NC:4 * NC:32], T.e6[:], shift(rank), None, A.add, after=[m2])
    need(g, "g", k1)
    g.remote_dma_fused([RemoteDMATransfer(dst_ids=[DstId(rid=topo.addr(dests[s])[0], pnc=topo.addr(dests[s])[1])], dma_engine_mask=sum(id_eng[s]),
                                          remote_sem=T.sem["id%d" % s], src=T["key%d" % s][:], dst=T["land%d" % s][:]) for s in (0, 1)], local_sem=T.sem.left)
    send(2, T.land2[:], T.key2[:], "id2", k2)

    sl = lambda s: slice(NC * s, NC * s + NC)
    scan = lambda s, d: vec(v.tensor_tensor_scan, T.zs[:, sl(s)], T.msk[:], T.z[:, sl(s)], 0.0, A.mult, A.add, after=[m3, d])
    turn = lambda s, d: vec(v.transpose, T.kb[:, sl(s)], T.zs[:, sl(s)], after=[d])

    def compare(s, d, bs=(0, 1, 2, 3)):
        for b in bs:
            last = vec(v.tensor_scalar, T.o[:, 768 * s + b:768 * s + 768:4], T.kb[:, sl(s)], T.sel[:, b:b + 1], None, A.is_equal, after=[d, ("gs", 1)])
        return last

    qo = lambda s, d: vec(v.quantize_mx, T.oc[:, sl(s)], T.op[:, sl(s)], T.o[:, 768 * s:768 * s + 768], after=[d])
    qe = lambda s, *d: vec(v.quantize_mx, T.ec[:, sl(s)], T.ep[:, sl(s)], T.e[:, 768 * s:768 * s + 768], after=d)
    qt = lambda f: vec(v.quantize_mx, T.tabc[:, 128 * f:128 * f + 128], T.tabp[:, 128 * f:128 * f + 128],
                       T.tabs[:, 512 * f:512 * f + 512], after=[("tl%d" % f, 16)])
    place = lambda s: vec(v.tensor_copy, T.z[:, NC * s:NC * s + NC:32], T["land%d" % s][:], after=[m2, ("id%d" % s, len(id_eng[s]))])

    def place_half(here, there):
        h = (slice(0, 64), slice(64, 128))
        first = 2 * NC + 96 * there
        return vec(v.tensor_copy, T.z[h[here], first:first + 96:32], T.land2[h[there], :], after=[("id2", len(id_eng[2]))])

    o_done, e_done = {}, {}
    o_done[3] = qo(3, compare(3, turn(3, scan(3, zown))))
    tab_done = [qt(f) for f in range(4)]

    p0 = place(0)
    p1 = place(1)
    s0 = scan(0, p0)
    s1 = scan(1, p1)
    t0 = turn(0, s0)
    t1 = turn(1, s1)
    c0 = compare(0, t0)
    compare(1, t1, (0,))
    o_done[0] = qo(0, c0)
    compare(1, t1, (1,))
    place_half(0, 0)
    place_half(1, 1)
    place_half(0, 1)
    p2 = place_half(1, 0)
    compare(1, t1, (2,))
    s2 = scan(2, p2)
    c1 = compare(1, t1, (3,))
    t2 = turn(2, s2)
    o_done[1] = qo(1, c1)
    c2 = compare(2, t2)

    order = (3, 0, 1, 2)
    e_copies = {}

    def product(m):
        s, f = order[m // 4], m % 4
        need(g.tensor, "t", tab_done[f], o_done[s])
        if m >= 7:
            need(g.tensor, "t", ("ss", m - 6))
        bank = 512 * (m % 7)
        g.tensor.matmul_mx(T.zp[:, bank:bank + NC], T.tabc[:, 128 * f:128 * f + 128], T.tabp[:, 128 * f:128 * f + 128],
                           T.oc[:, sl(s)], T.op[:, sl(s)], True, True).then_inc(T.sem.ps, 1)

    def sides(m):
        s, f, bank = order[m // 4], m % 4, 512 * (m % 7)
        return T.e[:, 768 * s + f:768 * s + 768:4], T.zp[:, bank:bank + NC]

    scalar_calls = [m for m in range(16) if m not in (13, 15)]
    for i, m in enumerate(scalar_calls):
        out, in_ = sides(m)
        need(g.scalar, "s", ("ps", m + 1))
        g.scalar.activation(out, in_, ActivationFunctionType.Copy).then_inc(T.sem.ss, 1)
        e_copies[m // 4] = ("ss", i + 1)

    e_done[0] = qe(0, e_copies[1])
    o_done[2] = qo(2, c2)
    e_done[1] = qe(1, e_copies[2])
    for m in (13, 15):
        out, in_ = sides(m)
        mine = vec(v.tensor_copy, out, in_, after=[("ps", m + 1)])
    e_done[2] = qe(2, e_copies[3], mine)
    w_done = vec(v.quantize_mx, T.wc[:], T.wp[:], T.wsb[:], after=[("wl", 16)])
    e_done[3] = qe(3, e_copies[0])

    for m in range(16):
        product(m)

    for s in range(3):
        send(s, T.lc[:, sl(s)].bitcast(dt.uint8), T.ec[:, sl(s)].bitcast(dt.uint8), "el%d" % s, e_done[s])
        send(s, T.lp[:, sl(s)], T.ep[:, sl(s)], "el%d" % s)

    need(g.tensor, "t", w_done, e_done[3])
    g.tensor.matmul_mx(T.yp[:, 0:NC], T.wc[:], T.wp[:], T.ec[:, sl(3)], T.ep[:, sl(3)], True, False)
    for s in range(3):
        need(g.tensor, "t", ("el%d" % s, 2 * len(eng[s])))
        mm = g.tensor.matmul_mx(T.yp[:, 0:NC], T.wc[:], T.wp[:], T.lc[:, sl(s)], T.lp[:, sl(s)], False, s == 2)
    mm.then_inc(T.sem.ps, 1)

    for k in range(6):
        fin = vec(v.tensor_copy, T.ysb[:, k:NC:6], T.yp[:, 32 * k:32 * k + 32], after=[("ps", 17)])
    need(g.sync, "y", fin)
    g.sync.dma_start(T.y[:], T.ysb[:]).then_inc(T.sem.st, 16)
    g.sync.wait_ge(T.sem.st, 16)
    g.wait_ge(T.sem.left, sum(len(x) for x in id_eng) + 2 * sum(len(x) for x in eng))
